import numpy as np, ml_dtypes
CORES = [211,219,227,235,243,251,83,91,99,107,115,123]
N = 12
F = 128
def setup_inputs(rng):
    return {"a": rng.standard_normal((N, 128, 128), dtype=np.float32).astype(ml_dtypes.bfloat16), "b": rng.standard_normal((N, 128, F), dtype=np.float32).astype(ml_dtypes.bfloat16)}
def setup_inputs_big(rng):
    d = setup_inputs(rng)
    for k in ("a", "b"): d[k] = (d[k].astype(np.float32) * 1024.0).astype(d[k].dtype)
    return d
def setup_inputs_small(rng):
    d = setup_inputs(rng)
    for k in ("a", "b"): d[k] = (d[k].astype(np.float32) * (1 / 1024.0)).astype(d[k].dtype)
    return d
def setup_inputs_apart(rng):
    d = setup_inputs(rng)
    f = (10.0 ** rng.permutation(np.linspace(-1.5, 1.5, N))).astype(np.float32).reshape(N, 1, 1)
    for k in ("a", "b"): d[k] = (d[k].astype(np.float32) * f).astype(d[k].dtype)
    return d
def reference(a, b):
    s = (a.astype(np.float64).sum(axis=0).T @ b.astype(np.float64).sum(axis=0)).astype(ml_dtypes.bfloat16 if a.dtype != np.float64 else np.float64)
    return {"y": np.broadcast_to(s, (N,) + s.shape)}

@@ -1,0 +1,162 @@
+from concourse.bass import DstId, RemoteDMATransfer
+
+N = 12
+NS = 8
+KR = 128 // NS
+G = 2
+NG = KR // G
+HALF = 64
+WA = G * 128
+
+SCRATCH = {
+    "src": ("dram", [NS, 128, 32], "bfloat16"),
+    "land": ("dram", [N - 1, 128, 32], "bfloat16"),
+    "full": ("dram", [NS, 128, 32], "bfloat16"),
+    "stack": ("sbuf", [128, 2 * WA], "bfloat16"),
+    "pat": ("sbuf", [128, NG * NG], "bfloat16"),
+    "sel": ("sbuf", [128, NG], "bfloat16"),
+    "ab": ("sbuf", [128, 2 * WA], "bfloat16"),
+    "ysb": ("sbuf", [128, 128], "bfloat16"),
+    "psa": ("psum", [128, 512], "float32"),
+    "psb": ("psum", [128, 512], "float32"),
+    "psy": ("psum", [128, 512], "float32"),
+}
+SEMAPHORES = ["ld", "own", "ms", "sl", "arr1", "arr2", "sent", "go", "stka", "stkb", "pea", "peb", "cp", "l2", "pey",
+              "cy", "st"]
+
+
+def _reducers(cores, topo):
+    first = cores[0]
+    pa = [c for c in cores if c == first or topo.same_plane(first, c)]
+    pb = [c for c in cores if c not in pa]
+    order = []
+    for i in range(max(len(pa), len(pb))):
+        order += pa[i:i + 1] + pb[i:i + 1]
+    return order[:NS]
+
+
+def _engines(core, dsts, topo):
+    m = topo.mask(core, dsts[0])
+    for d in dsts:
+        m &= topo.mask(core, d)
+    return [e for e in range(m.bit_length()) if (m >> e) & 1]
+
+
+def _scatter_plan(core, cores, red, topo):
+    ts = [t for t in range(NS) if red[t] != core]
+    eng = _engines(core, [c for c in cores if c != core], topo)
+    spare = len(eng) - len(ts)
+    plan, at = [], 0
+    for i, t in enumerate(ts):
+        n = 2 if i < spare else 1
+        mask = 0
+        for e in eng[at:at + n]:
+            mask |= 1 << e
+        at += n
+        plan.append((t, mask, n))
+    return plan
+
+
+def _slot(dst, t, red):
+    if dst in red and t < red.index(dst):
+        return t + 1
+    return t
+
+
+def rank_program(g, core, T, topo):
+    if T.rank_of(core) is None:
+        return
+    cores = list(T.cores)
+    others = [c for c in cores if c != core]
+    red = _reducers(cores, topo)
+    mine = red.index(core) if core in red else None
+    sem = T.sem
+    nst = (N - 1) * NG
+
+    g.sync.dma_start(out=T.src[:, 0:HALF, :], in_=T.a[:, :]).then_inc(sem.ld, 16)
+    g.scalar.dma_start(out=T.src[:, HALF:128, :], in_=T.b[:, :]).then_inc(sem.ld, 16)
+
+    if mine is not None:
+        k0 = mine * KR
+        g.sync.dma_start(out=T.stack[nst:nst + NG, 0:WA], in_=T.a[k0:k0 + KR, :]).then_inc(sem.own, 16)
+        g.scalar.dma_start(out=T.stack[nst:nst + NG, WA:2 * WA], in_=T.b[k0:k0 + KR, :]).then_inc(sem.own, 16)
+        g.vector.memset(T.pat[0:N, :], 0.0).then_inc(sem.ms, 1)
+        g.vector.wait_ge(sem.ms, 1)
+        for m in range(NG):
+            g.vector.memset(T.pat[0:N, m * (NG + 1):m * (NG + 1) + 1], 1.0).then_inc(sem.ms, 1)
+        g.sync.wait_ge(sem.ms, 1 + NG)
+        g.sync.dma_start(out=T.sel[0:N * NG, :], in_=T.pat[0:N, :]).then_inc(sem.sl, 16)
+
+    g.wait_ge(sem.ld, 32)
+    trs, sent = [], 0
+    for t, mask, n in _scatter_plan(core, cores, red, topo):
+        r = red[t]
+        rid, pid = topo.addr(r, core)
+        pos = [c for c in cores if c != r].index(core)
+        trs.append(RemoteDMATransfer(dst_ids=[DstId(rid=rid, pnc=pid)], dma_engine_mask=mask, remote_sem=sem.arr1,
+                                     src=T.src[t], dst=T.land[pos]))
+        sent += n
+    g.remote_dma_fused(trs, local_sem=sem.sent)
+
+    eng = _engines(core, others, topo)
+    if mine is not None:
+        e1 = 0
+        for c in others:
+            e1 += sum(n for t, mask, n in _scatter_plan(c, cores, red, topo) if t == mine)
+        allmask = 0
+        for e in eng:
+            allmask |= 1 << e
+        ids = []
+        for d in others:
+            rid, pid = topo.addr(d, core)
+            ids.append(DstId(rid=rid, pnc=pid))
+        g.wait_ge(sem.arr1, e1)
+        g.remote_dma_fused([RemoteDMATransfer(dst_ids=ids, dma_engine_mask=allmask, remote_sem=sem.arr2,
+                                              srcs=[T.land[i] for i in range(N - 1)] + [T.src[mine]],
+                                              dsts=[T.full[_slot(d, mine, red)] for d in others], alu_op=1)],
+                           local_sem=sem.sent)
+        sent += len(eng)
+        g.sem_inc(sem.go, 1)
+
+        g.sync.wait_ge(sem.arr1, e1)
+        g.sync.wait_ge(sem.go, 1)
+        g.sync.dma_start(out=T.stack[0:nst, 0:WA], in_=T.land[:, 0:HALF, :]).then_inc(sem.stka, 16)
+        g.scalar.wait_ge(sem.arr1, e1)
+        g.scalar.wait_ge(sem.go, 1)
+        g.scalar.dma_start(out=T.stack[0:nst, WA:2 * WA], in_=T.land[:, HALF:128, :]).then_inc(sem.stkb, 16)
+        np_ = N * NG
+        g.tensor.wait_ge(sem.sl, 16)
+        g.tensor.wait_ge(sem.own, 32)
+        g.tensor.wait_ge(sem.stka, 16)
+        g.tensor.matmul(T.psa[0:NG, 0:WA], T.sel[0:np_, :], T.stack[0:np_, 0:WA], True, True).then_inc(sem.pea, 1)
+        g.tensor.wait_ge(sem.stkb, 16)
+        g.tensor.matmul(T.psb[0:NG, 0:WA], T.sel[0:np_, :], T.stack[0:np_, WA:2 * WA], True, True).then_inc(sem.peb, 1)
+        g.vector.wait_ge(sem.pea, 1)
+        g.vector.tensor_copy(T.ab[0:NG, 0:WA], T.psa[0:NG, 0:WA]).then_inc(sem.cp, 1)
+        g.vector.wait_ge(sem.peb, 1)
+        g.vector.tensor_copy(T.ab[0:NG, WA:2 * WA], T.psb[0:NG, 0:WA]).then_inc(sem.cp, 1)
+
+    s0 = 0 if mine is None else 1
+    e2 = 0
+    for t in range(NS):
+        if red[t] != core:
+            e2 += len(_engines(red[t], [c for c in cores if c != red[t]], topo))
+    kp = NS * NG
+    g.sync.wait_ge(sem.arr2, e2)
+    g.sync.dma_start(out=T.ab[s0 * NG:kp, 0:WA], in_=T.full[s0:NS, 0:HALF, :]).then_inc(sem.l2, 16)
+    g.scalar.wait_ge(sem.arr2, e2)
+    g.scalar.dma_start(out=T.ab[s0 * NG:kp, WA:2 * WA], in_=T.full[s0:NS, HALF:128, :]).then_inc(sem.l2, 16)
+
+    g.tensor.wait_ge(sem.l2, 32)
+    if mine is not None:
+        g.tensor.wait_ge(sem.cp, 2)
+    for j in range(G):
+        mm = g.tensor.matmul(T.psy[:, 0:128], T.ab[0:kp, j * 128:(j + 1) * 128],
+                             T.ab[0:kp, WA + j * 128:WA + (j + 1) * 128], j == 0, j == G - 1)
+    mm.then_inc(sem.pey, 1)
+    g.vector.wait_ge(sem.pey, 1)
+    g.vector.tensor_copy(T.ysb[:, :], T.psy[:, 0:128]).then_inc(sem.cy, 1)
+    g.sync.wait_ge(sem.cy, 1)
+    g.sync.dma_start(out=T.y[:, :], in_=T.ysb[:, :]).then_inc(sem.st, 16)
+    g.sync.wait_ge(sem.st, 16)
+    g.wait_ge(sem.sent, sent)

@@ -1,28 +1,30 @@
 from concourse.bass import DstId, RemoteDMATransfer
 
 N = 12
-NS = 8
-KR = 128 // NS
+NT = (8, 4)
+KRT = (12, 8)
+K0T = (0, 96)
 G = 2
-NG = KR // G
+NGT = (KRT[0] // G, KRT[1] // G)
 HALF = 64
 WA = G * 128
 
 SCRATCH = {
-    "src": ("dram", [NS, 128, 32], "bfloat16"),
-    "land": ("dram", [N - 1, 128, 32], "bfloat16"),
-    "full": ("dram", [NS, 128, 32], "bfloat16"),
     "stack": ("sbuf", [128, 2 * WA], "bfloat16"),
-    "pat": ("sbuf", [128, NG * NG], "bfloat16"),
-    "sel": ("sbuf", [128, NG], "bfloat16"),
     "ab": ("sbuf", [128, 2 * WA], "bfloat16"),
     "ysb": ("sbuf", [128, 128], "bfloat16"),
     "psa": ("psum", [128, 512], "float32"),
     "psb": ("psum", [128, 512], "float32"),
     "psy": ("psum", [128, 512], "float32"),
 }
-SEMAPHORES = ["ld", "own", "ms", "sl", "arr1", "arr2", "sent", "go", "stka", "stkb", "pea", "peb", "cp", "l2", "pey",
-              "cy", "st"]
+for _k in range(2):
+    SCRATCH["src%d" % _k] = ("dram", [NT[_k], 128, 2 * KRT[_k]], "bfloat16")
+    SCRATCH["land%d" % _k] = ("dram", [N - 1, 128, 2 * KRT[_k]], "bfloat16")
+    SCRATCH["full%d" % _k] = ("dram", [NT[_k], 128, 2 * KRT[_k]], "bfloat16")
+    SCRATCH["pat%d" % _k] = ("sbuf", [128, NGT[_k] * NGT[_k]], "bfloat16")
+    SCRATCH["sel%d" % _k] = ("sbuf", [128, NGT[_k]], "bfloat16")
+SEMAPHORES = ["ld0", "ld1", "own", "ms", "sl", "arr1", "arr2", "sent", "go", "stka", "stkb", "pea", "peb", "cp", "l2",
+              "pey", "cy", "st"]
 
 
 def _reducers(cores, topo):
@@ -32,7 +34,7 @@ def _reducers(cores, topo):
     order = []
     for i in range(max(len(pa), len(pb))):
         order += pa[i:i + 1] + pb[i:i + 1]
-    return order[:NS]
+    return order[:NT[0]], order[NT[0]:]
 
 
 def _engines(core, dsts, topo):
@@ -42,25 +44,32 @@ def _engines(core, dsts, topo):
     return [e for e in range(m.bit_length()) if (m >> e) & 1]
 
 
-def _scatter_plan(core, cores, red, topo):
-    ts = [t for t in range(NS) if red[t] != core]
+def _scatter_plan(core, kind, cores, red, topo):
+    ts = [i for i in range(NT[kind]) if red[kind][i] != core]
     eng = _engines(core, [c for c in cores if c != core], topo)
-    spare = len(eng) - len(ts)
+    b = 1
+    while 2 * b * len(ts) <= len(eng):
+        b *= 2
+    ns = [b] * len(ts)
+    spare = len(eng) - b * len(ts)
+    for i in range(len(ts)):
+        if spare >= ns[i]:
+            spare -= ns[i]
+            ns[i] *= 2
     plan, at = [], 0
-    for i, t in enumerate(ts):
-        n = 2 if i < spare else 1
+    for i, n in zip(ts, ns):
         mask = 0
         for e in eng[at:at + n]:
             mask |= 1 << e
         at += n
-        plan.append((t, mask, n))
+        plan.append((i, mask, n))
     return plan
 
 
-def _slot(dst, t, red):
-    if dst in red and t < red.index(dst):
-        return t + 1
-    return t
+def _slot(dst, kind, i, red):
+    if dst in red[kind] and i < red[kind].index(dst):
+        return i + 1
+    return i
 
 
 def rank_program(g, core, T, topo):
@@ -69,87 +78,98 @@ def rank_program(g, core, T, topo):
     cores = list(T.cores)
     others = [c for c in cores if c != core]
     red = _reducers(cores, topo)
-    mine = red.index(core) if core in red else None
+    kd = 0 if core in red[0] else 1
+    ot = 1 - kd
+    mine = red[kd].index(core)
+    NG, KR = NGT[kd], KRT[kd]
     sem = T.sem
     nst = (N - 1) * NG
+    src = (T.src0, T.src1)
+    full = (T.full0, T.full1)
+    land = (T.land0, T.land1)[kd]
+    pat = (T.pat0, T.pat1)[kd]
+    sel = (T.sel0, T.sel1)[kd]
+    ld = (sem.ld0, sem.ld1)
 
-    g.sync.dma_start(out=T.src[:, 0:HALF, :], in_=T.a[:, :]).then_inc(sem.ld, 16)
-    g.scalar.dma_start(out=T.src[:, HALF:128, :], in_=T.b[:, :]).then_inc(sem.ld, 16)
+    for k in range(2):
+        r0, r1 = K0T[k], K0T[k] + NT[k] * KRT[k]
+        g.sync.dma_start(out=src[k][:, 0:HALF, :], in_=T.a[r0:r1, :]).then_inc(ld[k], 16)
+        g.scalar.dma_start(out=src[k][:, HALF:128, :], in_=T.b[r0:r1, :]).then_inc(ld[k], 16)
 
-    if mine is not None:
-        k0 = mine * KR
-        g.sync.dma_start(out=T.stack[nst:nst + NG, 0:WA], in_=T.a[k0:k0 + KR, :]).then_inc(sem.own, 16)
-        g.scalar.dma_start(out=T.stack[nst:nst + NG, WA:2 * WA], in_=T.b[k0:k0 + KR, :]).then_inc(sem.own, 16)
-        g.vector.memset(T.pat[0:N, :], 0.0).then_inc(sem.ms, 1)
-        g.vector.wait_ge(sem.ms, 1)
-        for m in range(NG):
-            g.vector.memset(T.pat[0:N, m * (NG + 1):m * (NG + 1) + 1], 1.0).then_inc(sem.ms, 1)
-        g.sync.wait_ge(sem.ms, 1 + NG)
-        g.sync.dma_start(out=T.sel[0:N * NG, :], in_=T.pat[0:N, :]).then_inc(sem.sl, 16)
+    k0 = K0T[kd] + mine * KR
+    g.sync.dma_start(out=T.stack[nst:nst + NG, 0:WA], in_=T.a[k0:k0 + KR, :]).then_inc(sem.own, 16)
+    g.scalar.dma_start(out=T.stack[nst:nst + NG, WA:2 * WA], in_=T.b[k0:k0 + KR, :]).then_inc(sem.own, 16)
+    g.vector.memset(pat[0:N, :], 0.0).then_inc(sem.ms, 1)
+    g.vector.wait_ge(sem.ms, 1)
+    for m in range(NG):
+        g.vector.memset(pat[0:N, m * (NG + 1):m * (NG + 1) + 1], 1.0).then_inc(sem.ms, 1)
+    g.sync.wait_ge(sem.ms, 1 + NG)
+    g.sync.dma_start(out=sel[0:N * NG, :], in_=pat[0:N, :]).then_inc(sem.sl, 16)
 
-    g.wait_ge(sem.ld, 32)
-    trs, sent = [], 0
-    for t, mask, n in _scatter_plan(core, cores, red, topo):
-        r = red[t]
-        rid, pid = topo.addr(r, core)
-        pos = [c for c in cores if c != r].index(core)
-        trs.append(RemoteDMATransfer(dst_ids=[DstId(rid=rid, pnc=pid)], dma_engine_mask=mask, remote_sem=sem.arr1,
-                                     src=T.src[t], dst=T.land[pos]))
-        sent += n
-    g.remote_dma_fused(trs, local_sem=sem.sent)
+    sent = 0
+    for k in range(2):
+        g.wait_ge(ld[k], 32)
+        trs = []
+        for i, mask, n in _scatter_plan(core, k, cores, red, topo):
+            r = red[k][i]
+            rid, pid = topo.addr(r, core)
+            pos = [c for c in cores if c != r].index(core)
+            trs.append(RemoteDMATransfer(dst_ids=[DstId(rid=rid, pnc=pid)], dma_engine_mask=mask, remote_sem=sem.arr1,
+                                         src=src[k][i], dst=(T.land0, T.land1)[k][pos]))
+            sent += n
+        g.remote_dma_fused(trs, local_sem=sem.sent)
 
     eng = _engines(core, others, topo)
-    if mine is not None:
-        e1 = 0
-        for c in others:
-            e1 += sum(n for t, mask, n in _scatter_plan(c, cores, red, topo) if t == mine)
-        allmask = 0
-        for e in eng:
-            allmask |= 1 << e
-        ids = []
-        for d in others:
-            rid, pid = topo.addr(d, core)
-            ids.append(DstId(rid=rid, pnc=pid))
-        g.wait_ge(sem.arr1, e1)
-        g.remote_dma_fused([RemoteDMATransfer(dst_ids=ids, dma_engine_mask=allmask, remote_sem=sem.arr2,
-                                              srcs=[T.land[i] for i in range(N - 1)] + [T.src[mine]],
-                                              dsts=[T.full[_slot(d, mine, red)] for d in others], alu_op=1)],
-                           local_sem=sem.sent)
-        sent += len(eng)
-        g.sem_inc(sem.go, 1)
+    e1 = 0
+    for c in others:
+        e1 += sum(n for i, mask, n in _scatter_plan(c, kd, cores, red, topo) if i == mine)
+    allmask = 0
+    for e in eng:
+        allmask |= 1 << e
+    ids = []
+    for d in others:
+        rid, pid = topo.addr(d, core)
+        ids.append(DstId(rid=rid, pnc=pid))
+    g.wait_ge(sem.arr1, e1)
+    g.remote_dma_fused([RemoteDMATransfer(dst_ids=ids, dma_engine_mask=allmask, remote_sem=sem.arr2,
+                                          srcs=[land[i] for i in range(N - 1)] + [src[kd][mine]],
+                                          dsts=[full[kd][_slot(d, kd, mine, red)] for d in others], alu_op=1)],
+                       local_sem=sem.sent)
+    sent += len(eng)
+    g.sem_inc(sem.go, 1)
 
-        g.sync.wait_ge(sem.arr1, e1)
-        g.sync.wait_ge(sem.go, 1)
-        g.sync.dma_start(out=T.stack[0:nst, 0:WA], in_=T.land[:, 0:HALF, :]).then_inc(sem.stka, 16)
-        g.scalar.wait_ge(sem.arr1, e1)
-        g.scalar.wait_ge(sem.go, 1)
-        g.scalar.dma_start(out=T.stack[0:nst, WA:2 * WA], in_=T.land[:, HALF:128, :]).then_inc(sem.stkb, 16)
-        np_ = N * NG
-        g.tensor.wait_ge(sem.sl, 16)
-        g.tensor.wait_ge(sem.own, 32)
-        g.tensor.wait_ge(sem.stka, 16)
-        g.tensor.matmul(T.psa[0:NG, 0:WA], T.sel[0:np_, :], T.stack[0:np_, 0:WA], True, True).then_inc(sem.pea, 1)
-        g.tensor.wait_ge(sem.stkb, 16)
-        g.tensor.matmul(T.psb[0:NG, 0:WA], T.sel[0:np_, :], T.stack[0:np_, WA:2 * WA], True, True).then_inc(sem.peb, 1)
-        g.vector.wait_ge(sem.pea, 1)
-        g.vector.tensor_copy(T.ab[0:NG, 0:WA], T.psa[0:NG, 0:WA]).then_inc(sem.cp, 1)
-        g.vector.wait_ge(sem.peb, 1)
-        g.vector.tensor_copy(T.ab[0:NG, WA:2 * WA], T.psb[0:NG, 0:WA]).then_inc(sem.cp, 1)
+    g.sync.wait_ge(sem.arr1, e1)
+    g.sync.wait_ge(sem.go, 1)
+    g.sync.dma_start(out=T.stack[0:nst, 0:WA], in_=land[:, 0:HALF, :]).then_inc(sem.stka, 16)
+    g.scalar.wait_ge(sem.arr1, e1)
+    g.scalar.wait_ge(sem.go, 1)
+    g.scalar.dma_start(out=T.stack[0:nst, WA:2 * WA], in_=land[:, HALF:128, :]).then_inc(sem.stkb, 16)
+    np_ = N * NG
+    g.tensor.wait_ge(sem.sl, 16)
+    g.tensor.wait_ge(sem.own, 32)
+    g.tensor.wait_ge(sem.stka, 16)
+    g.tensor.matmul(T.psa[0:NG, 0:WA], sel[0:np_, :], T.stack[0:np_, 0:WA], True, True).then_inc(sem.pea, 1)
+    g.tensor.wait_ge(sem.stkb, 16)
+    g.tensor.matmul(T.psb[0:NG, 0:WA], sel[0:np_, :], T.stack[0:np_, WA:2 * WA], True, True).then_inc(sem.peb, 1)
+    g.vector.wait_ge(sem.pea, 1)
+    g.vector.tensor_copy(T.ab[0:NG, 0:WA], T.psa[0:NG, 0:WA]).then_inc(sem.cp, 1)
+    g.vector.wait_ge(sem.peb, 1)
+    g.vector.tensor_copy(T.ab[0:NG, WA:2 * WA], T.psb[0:NG, 0:WA]).then_inc(sem.cp, 1)
 
-    s0 = 0 if mine is None else 1
     e2 = 0
-    for t in range(NS):
-        if red[t] != core:
-            e2 += len(_engines(red[t], [c for c in cores if c != red[t]], topo))
-    kp = NS * NG
+    for c in others:
+        e2 += len(_engines(c, [d for d in cores if d != c], topo))
+    p1 = NG * NT[kd]
+    kp = p1 + NGT[ot] * NT[ot]
     g.sync.wait_ge(sem.arr2, e2)
-    g.sync.dma_start(out=T.ab[s0 * NG:kp, 0:WA], in_=T.full[s0:NS, 0:HALF, :]).then_inc(sem.l2, 16)
+    g.sync.dma_start(out=T.ab[NG:p1, 0:WA], in_=full[kd][1:NT[kd], 0:HALF, :]).then_inc(sem.l2, 16)
+    g.sync.dma_start(out=T.ab[p1:kp, 0:WA], in_=full[ot][:, 0:HALF, :]).then_inc(sem.l2, 16)
     g.scalar.wait_ge(sem.arr2, e2)
-    g.scalar.dma_start(out=T.ab[s0 * NG:kp, WA:2 * WA], in_=T.full[s0:NS, HALF:128, :]).then_inc(sem.l2, 16)
+    g.scalar.dma_start(out=T.ab[NG:p1, WA:2 * WA], in_=full[kd][1:NT[kd], HALF:128, :]).then_inc(sem.l2, 16)
+    g.scalar.dma_start(out=T.ab[p1:kp, WA:2 * WA], in_=full[ot][:, HALF:128, :]).then_inc(sem.l2, 16)
 
-    g.tensor.wait_ge(sem.l2, 32)
-    if mine is not None:
-        g.tensor.wait_ge(sem.cp, 2)
+    g.tensor.wait_ge(sem.l2, 64)
+    g.tensor.wait_ge(sem.cp, 2)
     for j in range(G):
         mm = g.tensor.matmul(T.psy[:, 0:128], T.ab[0:kp, j * 128:(j + 1) * 128],
                              T.ab[0:kp, WA + j * 128:WA + (j + 1) * 128], j == 0, j == G - 1)

from concourse.bass import DstId, RemoteDMATransfer

N = 12
NT = (8, 4)
KRT = (12, 8)
K0T = (0, 96)
G = 2
NGT = (KRT[0] // G, KRT[1] // G)
HALF = 64
WA = G * 128

SCRATCH = {
    "stack": ("sbuf", [128, 2 * WA], "bfloat16"),
    "ab": ("sbuf", [128, 2 * WA], "bfloat16"),
    "ysb": ("sbuf", [128, 128], "bfloat16"),
    "psa": ("psum", [128, 512], "float32"),
    "psb": ("psum", [128, 512], "float32"),
    "psy": ("psum", [128, 512], "float32"),
}
for _k in range(2):
    SCRATCH["src%d" % _k] = ("dram", [NT[_k], 128, 2 * KRT[_k]], "bfloat16")
    SCRATCH["land%d" % _k] = ("dram", [N - 1, 128, 2 * KRT[_k]], "bfloat16")
    SCRATCH["full%d" % _k] = ("dram", [NT[_k], 128, 2 * KRT[_k]], "bfloat16")
    SCRATCH["pat%d" % _k] = ("sbuf", [128, NGT[_k] * NGT[_k]], "bfloat16")
    SCRATCH["sel%d" % _k] = ("sbuf", [128, NGT[_k]], "bfloat16")
SEMAPHORES = ["ld0", "ld1", "own", "ms", "sl", "arr1", "arr2", "sent", "go", "stka", "stkb", "pea", "peb", "cp", "l2",
              "pey", "cy", "st"]


def _reducers(cores, topo):
    first = cores[0]
    pa = [c for c in cores if c == first or topo.same_plane(first, c)]
    pb = [c for c in cores if c not in pa]
    order = []
    for i in range(max(len(pa), len(pb))):
        order += pa[i:i + 1] + pb[i:i + 1]
    return order[:NT[0]], order[NT[0]:]


def _engines(core, dsts, topo):
    m = topo.mask(core, dsts[0])
    for d in dsts:
        m &= topo.mask(core, d)
    return [e for e in range(m.bit_length()) if (m >> e) & 1]


def _scatter_plan(core, kind, cores, red, topo):
    ts = [i for i in range(NT[kind]) if red[kind][i] != core]
    eng = _engines(core, [c for c in cores if c != core], topo)
    b = 1
    while 2 * b * len(ts) <= len(eng):
        b *= 2
    ns = [b] * len(ts)
    spare = len(eng) - b * len(ts)
    for i in range(len(ts)):
        if spare >= ns[i]:
            spare -= ns[i]
            ns[i] *= 2
    plan, at = [], 0
    for i, n in zip(ts, ns):
        mask = 0
        for e in eng[at:at + n]:
            mask |= 1 << e
        at += n
        plan.append((i, mask, n))
    return plan


def _slot(dst, kind, i, red):
    if dst in red[kind] and i < red[kind].index(dst):
        return i + 1
    return i


def rank_program(g, core, T, topo):
    if T.rank_of(core) is None:
        return
    cores = list(T.cores)
    others = [c for c in cores if c != core]
    red = _reducers(cores, topo)
    kd = 0 if core in red[0] else 1
    ot = 1 - kd
    mine = red[kd].index(core)
    NG, KR = NGT[kd], KRT[kd]
    sem = T.sem
    nst = (N - 1) * NG
    src = (T.src0, T.src1)
    full = (T.full0, T.full1)
    land = (T.land0, T.land1)[kd]
    pat = (T.pat0, T.pat1)[kd]
    sel = (T.sel0, T.sel1)[kd]
    ld = (sem.ld0, sem.ld1)

    for k in range(2):
        r0, r1 = K0T[k], K0T[k] + NT[k] * KRT[k]
        g.sync.dma_start(out=src[k][:, 0:HALF, :], in_=T.a[r0:r1, :]).then_inc(ld[k], 16)
        g.scalar.dma_start(out=src[k][:, HALF:128, :], in_=T.b[r0:r1, :]).then_inc(ld[k], 16)

    k0 = K0T[kd] + mine * KR
    g.sync.dma_start(out=T.stack[nst:nst + NG, 0:WA], in_=T.a[k0:k0 + KR, :]).then_inc(sem.own, 16)
    g.scalar.dma_start(out=T.stack[nst:nst + NG, WA:2 * WA], in_=T.b[k0:k0 + KR, :]).then_inc(sem.own, 16)
    g.vector.memset(pat[0:N, :], 0.0).then_inc(sem.ms, 1)
    g.vector.wait_ge(sem.ms, 1)
    for m in range(NG):
        g.vector.memset(pat[0:N, m * (NG + 1):m * (NG + 1) + 1], 1.0).then_inc(sem.ms, 1)
    g.sync.wait_ge(sem.ms, 1 + NG)
    g.sync.dma_start(out=sel[0:N * NG, :], in_=pat[0:N, :]).then_inc(sem.sl, 16)

    sent = 0
    for k in range(2):
        g.wait_ge(ld[k], 32)
        trs = []
        for i, mask, n in _scatter_plan(core, k, cores, red, topo):
            r = red[k][i]
            rid, pid = topo.addr(r, core)
            pos = [c for c in cores if c != r].index(core)
            trs.append(RemoteDMATransfer(dst_ids=[DstId(rid=rid, pnc=pid)], dma_engine_mask=mask, remote_sem=sem.arr1,
                                         src=src[k][i], dst=(T.land0, T.land1)[k][pos]))
            sent += n
        g.remote_dma_fused(trs, local_sem=sem.sent)

    eng = _engines(core, others, topo)
    e1 = 0
    for c in others:
        e1 += sum(n for i, mask, n in _scatter_plan(c, kd, cores, red, topo) if i == mine)
    allmask = 0
    for e in eng:
        allmask |= 1 << e
    ids = []
    for d in others:
        rid, pid = topo.addr(d, core)
        ids.append(DstId(rid=rid, pnc=pid))
    g.wait_ge(sem.arr1, e1)
    g.remote_dma_fused([RemoteDMATransfer(dst_ids=ids, dma_engine_mask=allmask, remote_sem=sem.arr2,
                                          srcs=[land[i] for i in range(N - 1)] + [src[kd][mine]],
                                          dsts=[full[kd][_slot(d, kd, mine, red)] for d in others], alu_op=1)],
                       local_sem=sem.sent)
    sent += len(eng)
    g.sem_inc(sem.go, 1)

    g.sync.wait_ge(sem.arr1, e1)
    g.sync.wait_ge(sem.go, 1)
    g.sync.dma_start(out=T.stack[0:nst, 0:WA], in_=land[:, 0:HALF, :]).then_inc(sem.stka, 16)
    g.scalar.wait_ge(sem.arr1, e1)
    g.scalar.wait_ge(sem.go, 1)
    g.scalar.dma_start(out=T.stack[0:nst, WA:2 * WA], in_=land[:, HALF:128, :]).then_inc(sem.stkb, 16)
    np_ = N * NG
    g.tensor.wait_ge(sem.sl, 16)
    g.tensor.wait_ge(sem.own, 32)
    g.tensor.wait_ge(sem.stka, 16)
    g.tensor.matmul(T.psa[0:NG, 0:WA], sel[0:np_, :], T.stack[0:np_, 0:WA], True, True).then_inc(sem.pea, 1)
    g.tensor.wait_ge(sem.stkb, 16)
    g.tensor.matmul(T.psb[0:NG, 0:WA], sel[0:np_, :], T.stack[0:np_, WA:2 * WA], True, True).then_inc(sem.peb, 1)
    g.vector.wait_ge(sem.pea, 1)
    g.vector.tensor_copy(T.ab[0:NG, 0:WA], T.psa[0:NG, 0:WA]).then_inc(sem.cp, 1)
    g.vector.wait_ge(sem.peb, 1)
    g.vector.tensor_copy(T.ab[0:NG, WA:2 * WA], T.psb[0:NG, 0:WA]).then_inc(sem.cp, 1)

    e2 = 0
    for c in others:
        e2 += len(_engines(c, [d for d in cores if d != c], topo))
    p1 = NG * NT[kd]
    kp = p1 + NGT[ot] * NT[ot]
    g.sync.wait_ge(sem.arr2, e2)
    g.sync.dma_start(out=T.ab[NG:p1, 0:WA], in_=full[kd][1:NT[kd], 0:HALF, :]).then_inc(sem.l2, 16)
    g.sync.dma_start(out=T.ab[p1:kp, 0:WA], in_=full[ot][:, 0:HALF, :]).then_inc(sem.l2, 16)
    g.scalar.wait_ge(sem.arr2, e2)
    g.scalar.dma_start(out=T.ab[NG:p1, WA:2 * WA], in_=full[kd][1:NT[kd], HALF:128, :]).then_inc(sem.l2, 16)
    g.scalar.dma_start(out=T.ab[p1:kp, WA:2 * WA], in_=full[ot][:, HALF:128, :]).then_inc(sem.l2, 16)

    g.tensor.wait_ge(sem.l2, 64)
    g.tensor.wait_ge(sem.cp, 2)
    for j in range(G):
        mm = g.tensor.matmul(T.psy[:, 0:128], T.ab[0:kp, j * 128:(j + 1) * 128],
                             T.ab[0:kp, WA + j * 128:WA + (j + 1) * 128], j == 0, j == G - 1)
    mm.then_inc(sem.pey, 1)
    g.vector.wait_ge(sem.pey, 1)
    g.vector.tensor_copy(T.ysb[:, :], T.psy[:, 0:128]).then_inc(sem.cy, 1)
    g.sync.wait_ge(sem.cy, 1)
    g.sync.dma_start(out=T.y[:, :], in_=T.ysb[:, :]).then_inc(sem.st, 16)
    g.sync.wait_ge(sem.st, 16)
    g.wait_ge(sem.sent, sent)
